import numpy as np
import ml_dtypes


def mxq(x, axis, fmt="e4m3"):
    dtype, down = {"e4m3": (ml_dtypes.float8_e4m3fn, 7), "e5m2": (ml_dtypes.float8_e5m2, 14)}[fmt]
    v = np.moveaxis(np.asarray(x, np.float32).astype(ml_dtypes.bfloat16).astype(np.float64), axis, -1)
    blocks = v.reshape(v.shape[:-1] + (-1, 32))
    amax = np.abs(blocks).max(-1, keepdims=True)
    byte = np.maximum(np.where(amax > 0, np.frexp(amax)[1] - 1 + 127, 0) - down, 1)
    scale = np.exp2(byte - 127.0)
    codes = (blocks / scale).astype(np.float32).astype(dtype).astype(np.float64)
    return np.moveaxis((codes * scale).reshape(v.shape), -1, axis)


WIDE = False


def mx_kscale(k):
    if not WIDE:
        return np.ones(k)
    levels = np.array([10, -10, 5, -5, 0])
    if k % 512:
        return np.exp2(np.random.permutation(np.resize(levels, k // 32))).repeat(32)
    a = np.empty((k // 512, 16))
    for p in range(k // 512):
        a[p, :8] = np.random.permutation(np.resize(levels, 8))
        for g in range(8):
            far = levels[np.abs(levels - a[p, g]) >= 10]
            a[p, g + 8] = far[np.random.randint(len(far))]
    return np.exp2(a.ravel()).repeat(32)


def f64(x):
    return np.asarray(x).astype(np.float64)


def striped(idx):
    return np.tile(idx.reshape(-1, 16).T, (8, 1)).astype(np.uint16)


def unstriped(offs):
    return offs[:16].T.reshape(-1).astype(np.int64)


def relu(v):
    return np.maximum(v, 0.0)


K, T, E, C, H, N = 512, 512, 8, 128, 1024, 128


def by_expert(wq, xq):
    return np.concatenate([wq[e].T @ xq[:, e * C:(e + 1) * C] for e in range(E)], axis=1)


def setup_inputs():
    n = np.random.standard_normal
    s = mx_kscale(K)[:, None]
    u = mx_kscale(H)
    first = np.random.permutation(np.repeat(np.arange(E), T // E))
    second = (first + 1 + np.random.permutation(np.repeat(np.arange(E - 1), -(-T // (E - 1)))[:T])) % E
    while np.bincount(second, minlength=E).max() != T // E:
        load = np.bincount(second, minlength=E); hi, lo = int(load.argmax()), int(load.argmin())
        t = np.flatnonzero((second == hi) & (first != lo))[0]; second[t] = lo
    slot_token = np.empty(E * C, np.int64); pos = np.empty((2, T), np.int64); fill = np.zeros(E, np.int64)
    place = np.stack([np.random.permutation(C) for _ in range(E)])
    for r, deal in enumerate((first, second)):
        for t in np.random.permutation(T):
            e = deal[t]; j = e * C + place[e, fill[e]]; fill[e] += 1; slot_token[j] = t; pos[r, t] = j
    g = np.random.uniform(0.2, 0.8, T)
    return {
        "xT": (n((K, T)) * s).astype(np.float32),
        "w1": (n((E, K, H)) / np.sqrt(K) / s[None] * u[None, None, :]).astype(np.float32),
        "w2": (n((E, H, N)) / np.sqrt(H) / u[None, :, None]).astype(np.float32),
        "gate": np.stack([np.tile(g, (N, 1)), np.tile(1.0 - g, (N, 1))]).astype(np.float32),
        "offs": striped(slot_token),
        "pos1": striped(pos[0]),
        "pos2": striped(pos[1]),
    }


def reference(xT, w1, w2, gate, offs, pos1, pos2):
    idx = unstriped(offs)
    xq = mxq(f64(xT)[:, idx], 0, "e4m3")
    h = relu(by_expert(mxq(f64(w1), 1, "e4m3"), xq))
    y = by_expert(mxq(f64(w2), 1, "e4m3"), mxq(h, 0, "e4m3"))
    return f64(gate[0]) * y[:, unstriped(pos1)] + f64(gate[1]) * y[:, unstriped(pos2)]

@@ -1,0 +1,209 @@
+from contextlib import ExitStack
+
+import concourse.mybir as mybir
+
+F32 = mybir.dt.float32
+BF16 = mybir.dt.bfloat16
+U32 = mybir.dt.uint32
+U16 = mybir.dt.uint16
+U8 = mybir.dt.uint8
+FP8X4 = mybir.dt.float8_e4m3fn_x4
+RELU = mybir.ActivationFunctionType.Relu
+MULT = mybir.AluOpType.mult
+
+P = 128
+K, T, E, C, H, N = 512, 512, 8, 128, 1024, 128
+S = E * C
+HALF = 512
+FLOPS = 2 * S * K * H + 2 * S * H * N
+
+
+def tile_routed_moe_kernel(tc, xT, w1, w2, gate, offs, pos1, pos2, out):
+    nc = tc.nc
+    with ExitStack() as ctx:
+        keep = ctx.enter_context(tc.tile_pool(name="keep", bufs=1))
+        raw1 = ctx.enter_context(tc.tile_pool(name="raw1", bufs=8))
+        raw2 = ctx.enter_context(tc.tile_pool(name="raw2", bufs=8))
+        work = ctx.enter_context(tc.tile_pool(name="work", bufs=3))
+        hold = ctx.enter_context(tc.tile_pool(name="hold", bufs=4))
+        ps_a = ctx.enter_context(tc.psum_pool(name="ps_a", bufs=5))
+        ps_y = ctx.enter_context(tc.psum_pool(name="ps_y", bufs=2))
+
+        offs_t = keep.tile([P, S // 16], U16)
+        pos1_t = keep.tile([P, T // 16], U16)
+        pos2_t = keep.tile([P, T // 16], U16)
+        x_raw = keep.tile([P, 4, T], F32)
+        gate_t = keep.tile([P, 2, T], F32)
+        w1_raw = [raw1.tile([P, 4, H], F32, name="w1_raw") for e in range(E)]
+        w2_raw = [raw2.tile([P, 2, 4, N], F32, name="w2_raw") for e in range(E)]
+
+        def load_w1(e):
+            nc.sync.dma_start(out=w1_raw[e][:], in_=w1[e, :, :].rearrange("(p j) c -> p j c", j=4))
+
+        def load_w1_half(e, q):
+            cols = slice(q * HALF, (q + 1) * HALF)
+            nc.sync.dma_start(out=w1_raw[e][:, :, cols], in_=w1[e, :, cols].rearrange("(p j) c -> p j c", j=4))
+
+        def load_w2(e):
+            nc.sync.dma_start(out=w2_raw[e][:], in_=w2[e, :, :].rearrange("(q p j) n -> p q j n", p=P, j=4))
+
+        nc.sync.dma_start(out=x_raw[:], in_=xT.rearrange("(p j) t -> p j t", j=4))
+        nc.sync.dma_start(offs_t[:], offs)
+        load_w1(0)
+        load_w1(1)
+        load_w2(0)
+        load_w1(2)
+        load_w2(1)
+        load_w1(3)
+        load_w2(2)
+        load_w1(4)
+        load_w2(3)
+        load_w1(5)
+        load_w2(4)
+        load_w1_half(6, 0)
+        load_w1_half(6, 1)
+        load_w1_half(7, 0)
+        load_w1_half(7, 1)
+        load_w2(5)
+        load_w2(6)
+        nc.sync.dma_start(pos1_t[:], pos1)
+        nc.sync.dma_start(pos2_t[:], pos2)
+        load_w2(7)
+        nc.sync.dma_start(out=gate_t[:, 0, :], in_=gate[0, :, :])
+        nc.sync.dma_start(out=gate_t[:, 1, :], in_=gate[1, :, :])
+
+        x_bf = keep.tile([P, T, 4], BF16, align_bytes=64)
+        x_words = keep.tile([P, T], U32, align_bytes=64)
+        x_bytes = keep.tile([P, T], U8, align_bytes=64)
+        nc.gpsimd.memset(x_bytes[:], 0)
+        nc.vector.tensor_copy(out=x_bf[:, 0:352, :], in_=x_raw[:, :, 0:352].rearrange("p j t -> p t j"))
+        nc.scalar.copy(out=x_bf[:, 352:T, :], in_=x_raw[:, :, 352:T].rearrange("p j t -> p t j"))
+        nc.vector.quantize_mx(out=x_words[:].bitcast(FP8X4), scales=x_bytes[:], in_=x_bf[:].rearrange("p t j -> p (t j)"))
+        g_words = keep.tile([P, S], U32, align_bytes=64)
+        g_bytes = keep.tile([P, S], U8, align_bytes=64)
+
+        def gather(a, b):
+            lst = offs_t[:, a // 16:b // 16]
+            nc.vector.tensor_copy(g_words[:, a:b], x_words[:].indirect(lst))
+            nc.vector.tensor_copy(g_bytes[:, a:b], x_bytes[:].indirect(lst))
+
+        gather(0, 256)
+        gather(256, 640)
+        gather(640, 1024)
+
+        y_all = keep.tile([P, S], F32)
+
+        def cast_w1(e, q, split):
+            grouped = work.tile([P, 4, P, 4], BF16, name="w1_bf", align_bytes=64)
+            src = w1_raw[e][:, :, q * HALF:(q + 1) * HALF].rearrange("p j (m t) -> p m j t", t=4)
+            dst = grouped[:].rearrange("p t m j -> p m j t")
+            if split > 0:
+                nc.vector.tensor_copy(out=dst[:, 0:split], in_=src[:, 0:split])
+            if split < P:
+                nc.scalar.copy(out=dst[:, split:P], in_=src[:, split:P])
+            return grouped
+
+        def quant_w1(grouped):
+            words = work.tile([P, HALF], U32, name="w1_words", align_bytes=64)
+            scales = work.tile([P, HALF], U8, name="w1_scales", align_bytes=64)
+            nc.vector.quantize_mx(out=words[:].bitcast(FP8X4), scales=scales[:], in_=grouped[:].rearrange("p t m j -> p (t m j)"))
+            return words, scales
+
+        def cast_w2(e, split):
+            grouped = work.tile([P, 2, N, 4], BF16, name="w2_bf", align_bytes=64)
+            src = w2_raw[e][:].rearrange("p q j n -> p q n j")
+            if split > 0:
+                nc.vector.tensor_copy(out=grouped[:, 0:split], in_=src[:, 0:split])
+            if split < 2:
+                nc.scalar.copy(out=grouped[:, split:2], in_=src[:, split:2])
+            return grouped
+
+        def quant_w2(grouped):
+            words = work.tile([P, 2 * N], U32, name="w2_words", align_bytes=64)
+            scales = work.tile([P, 2 * N], U8, name="w2_scales", align_bytes=64)
+            nc.vector.quantize_mx(out=words[:].bitcast(FP8X4), scales=scales[:], in_=grouped[:].rearrange("p q n j -> p (q n j)"))
+            return words, scales
+
+        def layer1(e, q, w):
+            words, scales = w
+            bank = ps_a.tile([P, 4 * C], F32, name="h_bank")
+            slots = slice(e * C, (e + 1) * C)
+            for t in range(4):
+                cols = slice(t * P, (t + 1) * P)
+                nc.tensor.matmul_mx(
+                    out=bank[:, t * C:(t + 1) * C],
+                    lhsT=words[:, cols].bitcast(FP8X4), lhsT_scale=scales[:, cols],
+                    rhs=g_words[:, slots].bitcast(FP8X4), rhs_scale=g_bytes[:, slots],
+                    start=True, stop=True,
+                )
+            return bank
+
+        def relu(bank, h, q):
+            nc.scalar.activation(out=h[:, q], in_=bank[:].rearrange("p (t n) -> p n t", t=4), func=RELU)
+
+        def quant_h(h):
+            words = hold.tile([P, 2 * C], U32, name="h_words", align_bytes=64)
+            scales = hold.tile([P, 2 * C], U8, name="h_scales", align_bytes=64)
+            nc.vector.quantize_mx(out=words[:].bitcast(FP8X4), scales=scales[:], in_=h[:].rearrange("p q n t -> p (q n t)"))
+            return words, scales
+
+        def layer2(e, w, hq):
+            bank = ps_y.tile([P, C], F32, name="y_bank")
+            for q in range(2):
+                nc.tensor.matmul_mx(
+                    out=bank[:],
+                    lhsT=w[0][:, q * N:(q + 1) * N].bitcast(FP8X4), lhsT_scale=w[1][:, q * N:(q + 1) * N],
+                    rhs=hq[0][:, q * C:(q + 1) * C].bitcast(FP8X4), rhs_scale=hq[1][:, q * C:(q + 1) * C],
+                    start=(q == 0), stop=(q == 1),
+                )
+            nc.scalar.copy(out=y_all[:, e * C:(e + 1) * C], in_=bank[:])
+
+        def first(e, a, q, h):
+            relu(layer1(e, q, quant_w1(a)), h, q)
+
+        h_tiles = {}
+        h_codes = {}
+        for e in range(6):
+            a0 = cast_w1(e, 0, 0)
+            a1 = cast_w1(e, 1, P)
+            if e > 0:
+                h_codes[e - 1] = quant_h(h_tiles[e - 1])
+                g2 = cast_w2(e - 1, 2)
+            b1 = quant_w1(a1)
+            if e > 0:
+                c2 = quant_w2(g2)
+            b0 = quant_w1(a0)
+            h = work.tile([P, 2, C, 4], BF16, name="h_bf", align_bytes=64)
+            h_tiles[e] = h
+            relu(layer1(e, 1, b1), h, 1)
+            if e > 0:
+                layer2(e - 1, c2, h_codes[e - 1])
+            relu(layer1(e, 0, b0), h, 0)
+        for e, split0, split1 in ((6, 96, 64), (7, 96, 48)):
+            a0 = cast_w1(e, 0, split0)
+            h_codes[e - 1] = quant_h(h_tiles[e - 1])
+            b0 = quant_w1(a0)
+            a1 = cast_w1(e, 1, split1)
+            h = work.tile([P, 2, C, 4], BF16, name="h_bf", align_bytes=64)
+            h_tiles[e] = h
+            relu(layer1(e, 0, b0), h, 0)
+            if e == 7:
+                g5 = cast_w2(5, 2)
+            b1 = quant_w1(a1)
+            if e == 7:
+                layer2(5, quant_w2(g5), h_codes[5])
+                g6 = cast_w2(6, 2)
+            relu(layer1(e, 1, b1), h, 1)
+        c6 = quant_w2(g6)
+        h_codes[7] = quant_h(h_tiles[7])
+        layer2(6, c6, h_codes[6])
+        g7 = cast_w2(7, 1)
+        layer2(7, quant_w2(g7), h_codes[7])
+
+        part1 = keep.tile([P, T], F32)
+        part2 = keep.tile([P, T], F32)
+        result = keep.tile([P, T], F32)
+        nc.vector.tensor_tensor(part1[:], y_all[:].indirect(pos1_t[:]), gate_t[:, 0, :], MULT)
+        nc.vector.tensor_tensor(part2[:], y_all[:].indirect(pos2_t[:]), gate_t[:, 1, :], MULT)
+        nc.vector.tensor_add(result[:], part1[:], part2[:])
+        nc.sync.dma_start(out=out, in_=result[:])

@@ -76,8 +76,10 @@ def tile_routed_moe_kernel(tc, xT, w1, w2, gate, offs, pos1, pos2, out):
         x_words = keep.tile([P, T], U32, align_bytes=64)
         x_bytes = keep.tile([P, T], U8, align_bytes=64)
         nc.gpsimd.memset(x_bytes[:], 0)
-        nc.vector.tensor_copy(out=x_bf[:, 0:352, :], in_=x_raw[:, :, 0:352].rearrange("p j t -> p t j"))
-        nc.scalar.copy(out=x_bf[:, 352:T, :], in_=x_raw[:, :, 352:T].rearrange("p j t -> p t j"))
+        x_src = x_raw[:].rearrange("p j (c i) -> p c j i", i=4)
+        x_dst = x_bf[:].rearrange("p (c i) j -> p c j i", i=4)
+        nc.vector.tensor_copy(out=x_dst[:, 0:88], in_=x_src[:, 0:88])
+        nc.scalar.copy(out=x_dst[:, 88:128], in_=x_src[:, 88:128])
         nc.vector.quantize_mx(out=x_words[:].bitcast(FP8X4), scales=x_bytes[:], in_=x_bf[:].rearrange("p t j -> p (t j)"))
         g_words = keep.tile([P, S], U32, align_bytes=64)
         g_bytes = keep.tile([P, S], U8, align_bytes=64)
@@ -95,12 +97,12 @@ def tile_routed_moe_kernel(tc, xT, w1, w2, gate, offs, pos1, pos2, out):
 
         def cast_w1(e, q, split):
             grouped = work.tile([P, 4, P, 4], BF16, name="w1_bf", align_bytes=64)
-            src = w1_raw[e][:, :, q * HALF:(q + 1) * HALF].rearrange("p j (m t) -> p m j t", t=4)
-            dst = grouped[:].rearrange("p t m j -> p m j t")
+            src = w1_raw[e][:, :, q * HALF:(q + 1) * HALF].rearrange("p j (m u v) -> p u m j v", u=2, v=2)
+            dst = grouped[:].rearrange("p (u v) m j -> p u m j v", u=2)
             if split > 0:
-                nc.vector.tensor_copy(out=dst[:, 0:split], in_=src[:, 0:split])
+                nc.vector.tensor_copy(out=dst[:, :, 0:split], in_=src[:, :, 0:split])
             if split < P:
-                nc.scalar.copy(out=dst[:, split:P], in_=src[:, split:P])
+                nc.scalar.copy(out=dst[:, :, split:P], in_=src[:, :, split:P])
             return grouped
 
         def quant_w1(grouped):
@@ -111,11 +113,12 @@ def tile_routed_moe_kernel(tc, xT, w1, w2, gate, offs, pos1, pos2, out):
 
         def cast_w2(e, split):
             grouped = work.tile([P, 2, N, 4], BF16, name="w2_bf", align_bytes=64)
-            src = w2_raw[e][:].rearrange("p q j n -> p q n j")
+            src = w2_raw[e][:].rearrange("p q j (c i) -> p q c j i", i=4)
+            dst = grouped[:].rearrange("p q (c i) j -> p q c j i", i=4)
             if split > 0:
-                nc.vector.tensor_copy(out=grouped[:, 0:split], in_=src[:, 0:split])
+                nc.vector.tensor_copy(out=dst[:, 0:split], in_=src[:, 0:split])
             if split < 2:
-                nc.scalar.copy(out=grouped[:, split:2], in_=src[:, split:2])
+                nc.scalar.copy(out=dst[:, split:2], in_=src[:, split:2])
             return grouped
 
         def quant_w2(grouped):

@@ -15,6 +15,7 @@ P = 128
 K, T, E, C, H, N = 512, 512, 8, 128, 1024, 128
 S = E * C
 HALF = 512
+W2_LOADS = ((0, 2, 0), (2, 4, 4), (4, 5, 0), (5, 7, 4), (7, 8, 1))
 FLOPS = 2 * S * K * H + 2 * S * H * N
 
 
@@ -22,10 +23,9 @@ def tile_routed_moe_kernel(tc, xT, w1, w2, gate, offs, pos1, pos2, out):
     nc = tc.nc
     with ExitStack() as ctx:
         keep = ctx.enter_context(tc.tile_pool(name="keep", bufs=1))
-        raw1 = ctx.enter_context(tc.tile_pool(name="raw1", bufs=8))
-        raw2 = ctx.enter_context(tc.tile_pool(name="raw2", bufs=8))
+        raw = ctx.enter_context(tc.tile_pool(name="raw", bufs=16))
         work = ctx.enter_context(tc.tile_pool(name="work", bufs=3))
-        hold = ctx.enter_context(tc.tile_pool(name="hold", bufs=4))
+        hold = ctx.enter_context(tc.tile_pool(name="hold", bufs=8))
         ps_a = ctx.enter_context(tc.psum_pool(name="ps_a", bufs=5))
         ps_y = ctx.enter_context(tc.psum_pool(name="ps_y", bufs=2))
 
@@ -33,44 +33,23 @@ def tile_routed_moe_kernel(tc, xT, w1, w2, gate, offs, pos1, pos2, out):
         pos1_t = keep.tile([P, T // 16], U16)
         pos2_t = keep.tile([P, T // 16], U16)
         x_raw = keep.tile([P, 4, T], F32)
-        gate_t = keep.tile([P, 2, T], F32)
-        w1_raw = [raw1.tile([P, 4, H], F32, name="w1_raw") for e in range(E)]
-        w2_raw = [raw2.tile([P, 2, 4, N], F32, name="w2_raw") for e in range(E)]
-
-        def load_w1(e):
-            nc.sync.dma_start(out=w1_raw[e][:], in_=w1[e, :, :].rearrange("(p j) c -> p j c", j=4))
-
-        def load_w1_half(e, q):
-            cols = slice(q * HALF, (q + 1) * HALF)
-            nc.sync.dma_start(out=w1_raw[e][:, :, cols], in_=w1[e, :, cols].rearrange("(p j) c -> p j c", j=4))
-
-        def load_w2(e):
-            nc.sync.dma_start(out=w2_raw[e][:], in_=w2[e, :, :].rearrange("(q p j) n -> p q j n", p=P, j=4))
-
         nc.sync.dma_start(out=x_raw[:], in_=xT.rearrange("(p j) t -> p j t", j=4))
         nc.sync.dma_start(offs_t[:], offs)
-        load_w1(0)
-        load_w1(1)
-        load_w2(0)
-        load_w1(2)
-        load_w2(1)
-        load_w1(3)
-        load_w2(2)
-        load_w1(4)
-        load_w2(3)
-        load_w1(5)
-        load_w2(4)
-        load_w1_half(6, 0)
-        load_w1_half(6, 1)
-        load_w1_half(7, 0)
-        load_w1_half(7, 1)
-        load_w2(5)
-        load_w2(6)
         nc.sync.dma_start(pos1_t[:], pos1)
         nc.sync.dma_start(pos2_t[:], pos2)
-        load_w2(7)
-        nc.sync.dma_start(out=gate_t[:, 0, :], in_=gate[0, :, :])
-        nc.sync.dma_start(out=gate_t[:, 1, :], in_=gate[1, :, :])
+        w1_raw = {}
+        for e in range(E):
+            for q in range(2):
+                w1_raw[e, q] = raw.tile([P, 4, HALF], F32, name="raw")
+                src = w1[e, :, q * HALF:(q + 1) * HALF].rearrange("(p j) c -> p j c", j=4)
+                nc.sync.dma_start(out=w1_raw[e, q][:], in_=src)
+        w2_raw = {}
+        for a, b, split in W2_LOADS:
+            w2_raw[a] = raw.tile([P, 2 * (b - a), 4, N], F32, name="raw")
+            src = w2[a:b, :, :].rearrange("e (q p j) n -> p (e q) (j n)", p=P, j=4)
+            nc.sync.dma_start(out=w2_raw[a][:].rearrange("p q j n -> p q (j n)"), in_=src)
+        gate_t = raw.tile([P, 2, T], F32, name="raw")
+        nc.sync.dma_start(out=gate_t[:], in_=gate.rearrange("r p t -> p r t"))
 
         x_bf = keep.tile([P, T, 4], BF16, align_bytes=64)
         x_words = keep.tile([P, T], U32, align_bytes=64)
@@ -78,8 +57,8 @@ def tile_routed_moe_kernel(tc, xT, w1, w2, gate, offs, pos1, pos2, out):
         nc.gpsimd.memset(x_bytes[:], 0)
         x_src = x_raw[:].rearrange("p j (c i) -> p c j i", i=4)
         x_dst = x_bf[:].rearrange("p (c i) j -> p c j i", i=4)
-        nc.vector.tensor_copy(out=x_dst[:, 0:88], in_=x_src[:, 0:88])
-        nc.scalar.copy(out=x_dst[:, 88:128], in_=x_src[:, 88:128])
+        nc.vector.tensor_copy(out=x_dst[:, 0:64], in_=x_src[:, 0:64])
+        nc.scalar.copy(out=x_dst[:, 64:128], in_=x_src[:, 64:128])
         nc.vector.quantize_mx(out=x_words[:].bitcast(FP8X4), scales=x_bytes[:], in_=x_bf[:].rearrange("p t j -> p (t j)"))
         g_words = keep.tile([P, S], U32, align_bytes=64)
         g_bytes = keep.tile([P, S], U8, align_bytes=64)
@@ -89,41 +68,42 @@ def tile_routed_moe_kernel(tc, xT, w1, w2, gate, offs, pos1, pos2, out):
             nc.vector.tensor_copy(g_words[:, a:b], x_words[:].indirect(lst))
             nc.vector.tensor_copy(g_bytes[:, a:b], x_bytes[:].indirect(lst))
 
-        gather(0, 256)
-        gather(256, 640)
-        gather(640, 1024)
+        gathers = {0: (0, 256), 1: (256, 640), 2: (640, 1024)}
 
         y_all = keep.tile([P, S], F32)
 
-        def cast_w1(e, q, split):
-            grouped = work.tile([P, 4, P, 4], BF16, name="w1_bf", align_bytes=64)
-            src = w1_raw[e][:, :, q * HALF:(q + 1) * HALF].rearrange("p j (m u v) -> p u m j v", u=2, v=2)
-            dst = grouped[:].rearrange("p (u v) m j -> p u m j v", u=2)
-            if split > 0:
-                nc.vector.tensor_copy(out=dst[:, :, 0:split], in_=src[:, :, 0:split])
-            if split < P:
-                nc.scalar.copy(out=dst[:, :, split:P], in_=src[:, :, split:P])
-            return grouped
+        def cast_w1(e, grouped):
+            for q in range(2):
+                src = w1_raw[e, q][:].rearrange("p j (m u v) -> p u m j v", u=2, v=2)
+                dst = grouped[:, q].rearrange("p (u v) m j -> p u m j v", u=2)
+                if q == 0 or e == 0:
+                    nc.scalar.copy(out=dst, in_=src)
+                else:
+                    nc.vector.tensor_copy(out=dst, in_=src)
 
-        def quant_w1(grouped):
-            words = work.tile([P, HALF], U32, name="w1_words", align_bytes=64)
-            scales = work.tile([P, HALF], U8, name="w1_scales", align_bytes=64)
-            nc.vector.quantize_mx(out=words[:].bitcast(FP8X4), scales=scales[:], in_=grouped[:].rearrange("p t m j -> p (t m j)"))
+        def quant_w1(grouped, pieces):
+            words = work.tile([P, H], U32, name="w1_words", align_bytes=64, bufs=2)
+            scales = work.tile([P, H], U8, name="w1_scales", align_bytes=64, bufs=2)
+            flat = grouped[:].rearrange("p q t m j -> p (q t m j)")
+            step = H // pieces
+            for i in range(0, H, step):
+                cols = slice(i, i + step)
+                nc.vector.quantize_mx(out=words[:, cols].bitcast(FP8X4), scales=scales[:, cols], in_=flat[:, 4 * i:4 * (i + step)])
             return words, scales
 
-        def cast_w2(e, split):
-            grouped = work.tile([P, 2, N, 4], BF16, name="w2_bf", align_bytes=64)
-            src = w2_raw[e][:].rearrange("p q j (c i) -> p q c j i", i=4)
+        def cast_w2(a, b, split):
+            grouped = work.tile([P, 2 * (b - a), N, 4], BF16, name="grouped", align_bytes=64, bufs=2)
+            src = w2_raw[a][:].rearrange("p q j (c i) -> p q c j i", i=4)
             dst = grouped[:].rearrange("p q (c i) j -> p q c j i", i=4)
             if split > 0:
                 nc.vector.tensor_copy(out=dst[:, 0:split], in_=src[:, 0:split])
-            if split < 2:
-                nc.scalar.copy(out=dst[:, split:2], in_=src[:, split:2])
+            if split < 2 * (b - a):
+                nc.scalar.copy(out=dst[:, split:], in_=src[:, split:])
             return grouped
 
-        def quant_w2(grouped):
-            words = work.tile([P, 2 * N], U32, name="w2_words", align_bytes=64)
-            scales = work.tile([P, 2 * N], U8, name="w2_scales", align_bytes=64)
+        def quant_w2(grouped, n):
+            words = work.tile([P, n * N], U32, name="w2_words", align_bytes=64, bufs=2)
+            scales = work.tile([P, n * N], U8, name="w2_scales", align_bytes=64, bufs=2)
             nc.vector.quantize_mx(out=words[:].bitcast(FP8X4), scales=scales[:], in_=grouped[:].rearrange("p q n j -> p (q n j)"))
             return words, scales
 
@@ -132,7 +112,7 @@ def tile_routed_moe_kernel(tc, xT, w1, w2, gate, offs, pos1, pos2, out):
             bank = ps_a.tile([P, 4 * C], F32, name="h_bank")
             slots = slice(e * C, (e + 1) * C)
             for t in range(4):
-                cols = slice(t * P, (t + 1) * P)
+                cols = slice(q * HALF + t * P, q * HALF + (t + 1) * P)
                 nc.tensor.matmul_mx(
                     out=bank[:, t * C:(t + 1) * C],
                     lhsT=words[:, cols].bitcast(FP8X4), lhsT_scale=scales[:, cols],
@@ -150,58 +130,38 @@ def tile_routed_moe_kernel(tc, xT, w1, w2, gate, offs, pos1, pos2, out):
             nc.vector.quantize_mx(out=words[:].bitcast(FP8X4), scales=scales[:], in_=h[:].rearrange("p q n t -> p (q n t)"))
             return words, scales
 
-        def layer2(e, w, hq):
+        def layer2(e, w, first, hq):
             bank = ps_y.tile([P, C], F32, name="y_bank")
             for q in range(2):
+                cols = slice((first + q) * N, (first + q + 1) * N)
                 nc.tensor.matmul_mx(
                     out=bank[:],
-                    lhsT=w[0][:, q * N:(q + 1) * N].bitcast(FP8X4), lhsT_scale=w[1][:, q * N:(q + 1) * N],
+                    lhsT=w[0][:, cols].bitcast(FP8X4), lhsT_scale=w[1][:, cols],
                     rhs=hq[0][:, q * C:(q + 1) * C].bitcast(FP8X4), rhs_scale=hq[1][:, q * C:(q + 1) * C],
                     start=(q == 0), stop=(q == 1),
                 )
             nc.scalar.copy(out=y_all[:, e * C:(e + 1) * C], in_=bank[:])
 
-        def first(e, a, q, h):
-            relu(layer1(e, q, quant_w1(a)), h, q)
-
-        h_tiles = {}
-        h_codes = {}
-        for e in range(6):
-            a0 = cast_w1(e, 0, 0)
-            a1 = cast_w1(e, 1, P)
-            if e > 0:
-                h_codes[e - 1] = quant_h(h_tiles[e - 1])
-                g2 = cast_w2(e - 1, 2)
-            b1 = quant_w1(a1)
-            if e > 0:
-                c2 = quant_w2(g2)
-            b0 = quant_w1(a0)
-            h = work.tile([P, 2, C, 4], BF16, name="h_bf", align_bytes=64)
-            h_tiles[e] = h
-            relu(layer1(e, 1, b1), h, 1)
-            if e > 0:
-                layer2(e - 1, c2, h_codes[e - 1])
-            relu(layer1(e, 0, b0), h, 0)
-        for e, split0, split1 in ((6, 96, 64), (7, 96, 48)):
-            a0 = cast_w1(e, 0, split0)
-            h_codes[e - 1] = quant_h(h_tiles[e - 1])
-            b0 = quant_w1(a0)
-            a1 = cast_w1(e, 1, split1)
-            h = work.tile([P, 2, C, 4], BF16, name="h_bf", align_bytes=64)
-            h_tiles[e] = h
-            relu(layer1(e, 0, b0), h, 0)
-            if e == 7:
-                g5 = cast_w2(5, 2)
-            b1 = quant_w1(a1)
-            if e == 7:
-                layer2(5, quant_w2(g5), h_codes[5])
-                g6 = cast_w2(6, 2)
-            relu(layer1(e, 1, b1), h, 1)
-        c6 = quant_w2(g6)
-        h_codes[7] = quant_h(h_tiles[7])
-        layer2(6, c6, h_codes[6])
-        g7 = cast_w2(7, 1)
-        layer2(7, quant_w2(g7), h_codes[7])
+        h_codes = []
+        h = None
+        for e in range(E):
+            if e in gathers:
+                gather(*gathers[e])
+            grouped = work.tile([P, 2, 4, P, 4], BF16, name="grouped", align_bytes=64, bufs=2)
+            cast_w1(e, grouped)
+            w = quant_w1(grouped, 1)
+            if h is not None:
+                h_codes.append(quant_h(h))
+            h = work.tile([P, 2, C, 4], BF16, name="h_bf", align_bytes=64, bufs=2)
+            for q in range(2):
+                relu(layer1(e, q, w), h, q)
+        for a, b, split in W2_LOADS:
+            g = cast_w2(a, b, split)
+            if a == 0:
+                h_codes.append(quant_h(h))
+            w = quant_w2(g, 2 * (b - a))
+            for e in range(a, b):
+                layer2(e, w, 2 * (e - a), h_codes[e])
 
         part1 = keep.tile([P, T], F32)
         part2 = keep.tile([P, T], F32)

@@ -15,7 +15,7 @@ P = 128
 K, T, E, C, H, N = 512, 512, 8, 128, 1024, 128
 S = E * C
 HALF = 512
-W2_LOADS = ((0, 2, 0), (2, 4, 4), (4, 5, 0), (5, 7, 4), (7, 8, 1))
+W2_LOADS = ((0, 2, 4), (2, 4, 4), (4, 5, 0), (5, 7, 4), (7, 8, 0))
 FLOPS = 2 * S * K * H + 2 * S * H * N
 
 
@@ -23,7 +23,7 @@ def tile_routed_moe_kernel(tc, xT, w1, w2, gate, offs, pos1, pos2, out):
     nc = tc.nc
     with ExitStack() as ctx:
         keep = ctx.enter_context(tc.tile_pool(name="keep", bufs=1))
-        raw = ctx.enter_context(tc.tile_pool(name="raw", bufs=16))
+        raw = ctx.enter_context(tc.tile_pool(name="raw", bufs=8))
         work = ctx.enter_context(tc.tile_pool(name="work", bufs=3))
         hold = ctx.enter_context(tc.tile_pool(name="hold", bufs=8))
         ps_a = ctx.enter_context(tc.psum_pool(name="ps_a", bufs=5))
@@ -37,12 +37,11 @@ def tile_routed_moe_kernel(tc, xT, w1, w2, gate, offs, pos1, pos2, out):
         nc.sync.dma_start(offs_t[:], offs)
         nc.sync.dma_start(pos1_t[:], pos1)
         nc.sync.dma_start(pos2_t[:], pos2)
-        w1_raw = {}
+        w1_raw = []
         for e in range(E):
-            for q in range(2):
-                w1_raw[e, q] = raw.tile([P, 4, HALF], F32, name="raw")
-                src = w1[e, :, q * HALF:(q + 1) * HALF].rearrange("(p j) c -> p j c", j=4)
-                nc.sync.dma_start(out=w1_raw[e, q][:], in_=src)
+            tile = raw.tile([P, 4, H], F32, name="raw")
+            nc.sync.dma_start(out=tile[:], in_=w1[e, :, :].rearrange("(p j) c -> p j c", j=4))
+            w1_raw.append(tile)
         w2_raw = {}
         for a, b, split in W2_LOADS:
             w2_raw[a] = raw.tile([P, 2 * (b - a), 4, N], F32, name="raw")
@@ -72,27 +71,24 @@ def tile_routed_moe_kernel(tc, xT, w1, w2, gate, offs, pos1, pos2, out):
 
         y_all = keep.tile([P, S], F32)
 
-        def cast_w1(e, grouped):
-            for q in range(2):
-                src = w1_raw[e, q][:].rearrange("p j (m u v) -> p u m j v", u=2, v=2)
-                dst = grouped[:, q].rearrange("p (u v) m j -> p u m j v", u=2)
-                if q == 0 or e == 0:
-                    nc.scalar.copy(out=dst, in_=src)
-                else:
-                    nc.vector.tensor_copy(out=dst, in_=src)
+        def cast_w1(e, q):
+            grouped = work.tile([P, 4, P, 4], BF16, name="w1_bf", align_bytes=64)
+            src = w1_raw[e][:, :, q * HALF:(q + 1) * HALF].rearrange("p j (m u v) -> p u m j v", u=2, v=2)
+            dst = grouped[:].rearrange("p (u v) m j -> p u m j v", u=2)
+            if q == 0 or e == 0:
+                nc.scalar.copy(out=dst, in_=src)
+            else:
+                nc.vector.tensor_copy(out=dst, in_=src)
+            return grouped
 
-        def quant_w1(grouped, pieces):
-            words = work.tile([P, H], U32, name="w1_words", align_bytes=64, bufs=2)
-            scales = work.tile([P, H], U8, name="w1_scales", align_bytes=64, bufs=2)
-            flat = grouped[:].rearrange("p q t m j -> p (q t m j)")
-            step = H // pieces
-            for i in range(0, H, step):
-                cols = slice(i, i + step)
-                nc.vector.quantize_mx(out=words[:, cols].bitcast(FP8X4), scales=scales[:, cols], in_=flat[:, 4 * i:4 * (i + step)])
+        def quant_w1(grouped):
+            words = work.tile([P, HALF], U32, name="w1_words", align_bytes=64, bufs=4)
+            scales = work.tile([P, HALF], U8, name="w1_scales", align_bytes=64, bufs=4)
+            nc.vector.quantize_mx(out=words[:].bitcast(FP8X4), scales=scales[:], in_=grouped[:].rearrange("p t m j -> p (t m j)"))
             return words, scales
 
         def cast_w2(a, b, split):
-            grouped = work.tile([P, 2 * (b - a), N, 4], BF16, name="grouped", align_bytes=64, bufs=2)
+            grouped = work.tile([P, 2 * (b - a), N, 4], BF16, name="w2_bf", align_bytes=64, bufs=2)
             src = w2_raw[a][:].rearrange("p q j (c i) -> p q c j i", i=4)
             dst = grouped[:].rearrange("p q (c i) j -> p q c j i", i=4)
             if split > 0:
@@ -107,12 +103,12 @@ def tile_routed_moe_kernel(tc, xT, w1, w2, gate, offs, pos1, pos2, out):
             nc.vector.quantize_mx(out=words[:].bitcast(FP8X4), scales=scales[:], in_=grouped[:].rearrange("p q n j -> p (q n j)"))
             return words, scales
 
-        def layer1(e, q, w):
+        def layer1(e, w):
             words, scales = w
             bank = ps_a.tile([P, 4 * C], F32, name="h_bank")
             slots = slice(e * C, (e + 1) * C)
             for t in range(4):
-                cols = slice(q * HALF + t * P, q * HALF + (t + 1) * P)
+                cols = slice(t * P, (t + 1) * P)
                 nc.tensor.matmul_mx(
                     out=bank[:, t * C:(t + 1) * C],
                     lhsT=words[:, cols].bitcast(FP8X4), lhsT_scale=scales[:, cols],
@@ -121,8 +117,12 @@ def tile_routed_moe_kernel(tc, xT, w1, w2, gate, offs, pos1, pos2, out):
                 )
             return bank
 
-        def relu(bank, h, q):
-            nc.scalar.activation(out=h[:, q], in_=bank[:].rearrange("p (t n) -> p n t", t=4), func=RELU)
+        def relu(banks, zero):
+            h = work.tile([P, 2, C, 4], BF16, name="h_bf", align_bytes=64, bufs=2)
+            for q in range(2):
+                src = banks[q][:].rearrange("p (t n) -> p n t", t=4)
+                nc.scalar.activation(out=h[:, q], in_=src, func=RELU, bias=zero)
+            return h
 
         def quant_h(h):
             words = hold.tile([P, 2 * C], U32, name="h_words", align_bytes=64)
@@ -143,18 +143,19 @@ def tile_routed_moe_kernel(tc, xT, w1, w2, gate, offs, pos1, pos2, out):
             nc.scalar.copy(out=y_all[:, e * C:(e + 1) * C], in_=bank[:])
 
         h_codes = []
-        h = None
+        banks = None
         for e in range(E):
             if e in gathers:
                 gather(*gathers[e])
-            grouped = work.tile([P, 2, 4, P, 4], BF16, name="grouped", align_bytes=64, bufs=2)
-            cast_w1(e, grouped)
-            w = quant_w1(grouped, 1)
-            if h is not None:
-                h_codes.append(quant_h(h))
-            h = work.tile([P, 2, C, 4], BF16, name="h_bf", align_bytes=64, bufs=2)
-            for q in range(2):
-                relu(layer1(e, q, w), h, q)
+            halves = [cast_w1(e, q) for q in range(2)]
+            if e > 0:
+                zero = work.tile([P, 1], F32, name="zero")
+                nc.vector.tensor_scalar(out=zero[:], in0=halves[1][:, 3, P - 1, 3:4], scalar1=0.0, scalar2=None, op0=MULT)
+                h_codes.append(quant_h(relu(banks, zero[:])))
+            banks = {}
+            for q in (0, 1) if e < 6 else (1, 0):
+                banks[q] = layer1(e, quant_w1(halves[q]))
+        h = relu(banks, 0.0)
         for a, b, split in W2_LOADS:
             g = cast_w2(a, b, split)
             if a == 0:

@@ -10,6 +10,7 @@ U8 = mybir.dt.uint8
 FP8X4 = mybir.dt.float8_e4m3fn_x4
 RELU = mybir.ActivationFunctionType.Relu
 MULT = mybir.AluOpType.mult
+MAX = mybir.AluOpType.max
 
 P = 128
 K, T, E, C, H, N = 512, 512, 8, 128, 1024, 128
@@ -25,7 +26,7 @@ def tile_routed_moe_kernel(tc, xT, w1, w2, gate, offs, pos1, pos2, out):
         keep = ctx.enter_context(tc.tile_pool(name="keep", bufs=1))
         raw = ctx.enter_context(tc.tile_pool(name="raw", bufs=8))
         work = ctx.enter_context(tc.tile_pool(name="work", bufs=3))
-        hold = ctx.enter_context(tc.tile_pool(name="hold", bufs=8))
+        hold = ctx.enter_context(tc.tile_pool(name="hold", bufs=4))
         ps_a = ctx.enter_context(tc.psum_pool(name="ps_a", bufs=5))
         ps_y = ctx.enter_context(tc.psum_pool(name="ps_y", bufs=2))
 
@@ -37,11 +38,16 @@ def tile_routed_moe_kernel(tc, xT, w1, w2, gate, offs, pos1, pos2, out):
         nc.sync.dma_start(offs_t[:], offs)
         nc.sync.dma_start(pos1_t[:], pos1)
         nc.sync.dma_start(pos2_t[:], pos2)
-        w1_raw = []
+        w1_raw = {}
         for e in range(E):
-            tile = raw.tile([P, 4, H], F32, name="raw")
-            nc.sync.dma_start(out=tile[:], in_=w1[e, :, :].rearrange("(p j) c -> p j c", j=4))
-            w1_raw.append(tile)
+            parts = 2 if e == 0 else 1
+            width = H // parts
+            for i in range(parts):
+                tile = raw.tile([P, 4, width], F32, name="raw")
+                src = w1[e, :, i * width:(i + 1) * width].rearrange("(p j) c -> p j c", j=4)
+                nc.sync.dma_start(out=tile[:], in_=src)
+                for q in range(2 // parts):
+                    w1_raw[e, i + q] = tile[:, :, q * HALF:(q + 1) * HALF]
         w2_raw = {}
         for a, b, split in W2_LOADS:
             w2_raw[a] = raw.tile([P, 2 * (b - a), 4, N], F32, name="raw")
@@ -73,7 +79,7 @@ def tile_routed_moe_kernel(tc, xT, w1, w2, gate, offs, pos1, pos2, out):
 
         def cast_w1(e, q):
             grouped = work.tile([P, 4, P, 4], BF16, name="w1_bf", align_bytes=64)
-            src = w1_raw[e][:, :, q * HALF:(q + 1) * HALF].rearrange("p j (m u v) -> p u m j v", u=2, v=2)
+            src = w1_raw[e, q].rearrange("p j (m u v) -> p u m j v", u=2, v=2)
             dst = grouped[:].rearrange("p (u v) m j -> p u m j v", u=2)
             if q == 0 or e == 0:
                 nc.scalar.copy(out=dst, in_=src)
@@ -117,52 +123,59 @@ def tile_routed_moe_kernel(tc, xT, w1, w2, gate, offs, pos1, pos2, out):
                 )
             return bank
 
-        def relu(banks, zero):
-            h = work.tile([P, 2, C, 4], BF16, name="h_bf", align_bytes=64, bufs=2)
+        def relu(e, banks, h, zero):
             for q in range(2):
                 src = banks[q][:].rearrange("p (t n) -> p n t", t=4)
-                nc.scalar.activation(out=h[:, q], in_=src, func=RELU, bias=zero)
-            return h
+                if q == 1 and e in (1, 3, 5):
+                    nc.vector.tensor_scalar(out=h[:, e % 2, q], in0=src, scalar1=zero, scalar2=None, op0=MAX)
+                else:
+                    nc.scalar.activation(out=h[:, e % 2, q], in_=src, func=RELU, bias=zero)
 
         def quant_h(h):
-            words = hold.tile([P, 2 * C], U32, name="h_words", align_bytes=64)
-            scales = hold.tile([P, 2 * C], U8, name="h_scales", align_bytes=64)
-            nc.vector.quantize_mx(out=words[:].bitcast(FP8X4), scales=scales[:], in_=h[:].rearrange("p q n t -> p (q n t)"))
+            words = hold.tile([P, 4 * C], U32, name="h_words", align_bytes=64)
+            scales = hold.tile([P, 4 * C], U8, name="h_scales", align_bytes=64)
+            nc.vector.quantize_mx(out=words[:].bitcast(FP8X4), scales=scales[:], in_=h[:].rearrange("p e q n t -> p (e q n t)"))
             return words, scales
 
         def layer2(e, w, first, hq):
             bank = ps_y.tile([P, C], F32, name="y_bank")
             for q in range(2):
                 cols = slice((first + q) * N, (first + q + 1) * N)
+                slots = slice((2 * (e % 2) + q) * C, (2 * (e % 2) + q + 1) * C)
                 nc.tensor.matmul_mx(
                     out=bank[:],
                     lhsT=w[0][:, cols].bitcast(FP8X4), lhsT_scale=w[1][:, cols],
-                    rhs=hq[0][:, q * C:(q + 1) * C].bitcast(FP8X4), rhs_scale=hq[1][:, q * C:(q + 1) * C],
+                    rhs=hq[0][:, slots].bitcast(FP8X4), rhs_scale=hq[1][:, slots],
                     start=(q == 0), stop=(q == 1),
                 )
             nc.scalar.copy(out=y_all[:, e * C:(e + 1) * C], in_=bank[:])
 
         h_codes = []
-        banks = None
+        banks = {}
+        h = None
         for e in range(E):
             if e in gathers:
                 gather(*gathers[e])
             halves = [cast_w1(e, q) for q in range(2)]
             if e > 0:
                 zero = work.tile([P, 1], F32, name="zero")
-                nc.vector.tensor_scalar(out=zero[:], in0=halves[1][:, 3, P - 1, 3:4], scalar1=0.0, scalar2=None, op0=MULT)
-                h_codes.append(quant_h(relu(banks, zero[:])))
+                nc.gpsimd.tensor_scalar(out=zero[:], in0=halves[1][:, 3, P - 1, 3:4], scalar1=0.0, scalar2=None, op0=MULT)
+                if e % 2 == 1:
+                    h = work.tile([P, 2, 2, C, 4], BF16, name="h_bf", align_bytes=64, bufs=2)
+                relu(e - 1, banks, h, zero[:])
+                if e % 2 == 0:
+                    h_codes.append(quant_h(h))
             banks = {}
-            for q in (0, 1) if e < 6 else (1, 0):
+            for q in (1, 0):
                 banks[q] = layer1(e, quant_w1(halves[q]))
-        h = relu(banks, 0.0)
+        relu(E - 1, banks, h, 0.0)
         for a, b, split in W2_LOADS:
             g = cast_w2(a, b, split)
             if a == 0:
                 h_codes.append(quant_h(h))
             w = quant_w2(g, 2 * (b - a))
             for e in range(a, b):
-                layer2(e, w, 2 * (e - a), h_codes[e])
+                layer2(e, w, 2 * (e - a), h_codes[e // 2])
 
         part1 = keep.tile([P, T], F32)
         part2 = keep.tile([P, T], F32)

from contextlib import ExitStack

import concourse.mybir as mybir

F32 = mybir.dt.float32
BF16 = mybir.dt.bfloat16
U32 = mybir.dt.uint32
U16 = mybir.dt.uint16
U8 = mybir.dt.uint8
FP8X4 = mybir.dt.float8_e4m3fn_x4
RELU = mybir.ActivationFunctionType.Relu
MULT = mybir.AluOpType.mult
MAX = mybir.AluOpType.max

P = 128
K, T, E, C, H, N = 512, 512, 8, 128, 1024, 128
S = E * C
HALF = 512
W2_LOADS = ((0, 2, 4), (2, 4, 4), (4, 5, 0), (5, 7, 4), (7, 8, 0))
FLOPS = 2 * S * K * H + 2 * S * H * N


def tile_routed_moe_kernel(tc, xT, w1, w2, gate, offs, pos1, pos2, out):
    nc = tc.nc
    with ExitStack() as ctx:
        keep = ctx.enter_context(tc.tile_pool(name="keep", bufs=1))
        raw = ctx.enter_context(tc.tile_pool(name="raw", bufs=8))
        work = ctx.enter_context(tc.tile_pool(name="work", bufs=3))
        hold = ctx.enter_context(tc.tile_pool(name="hold", bufs=4))
        ps_a = ctx.enter_context(tc.psum_pool(name="ps_a", bufs=5))
        ps_y = ctx.enter_context(tc.psum_pool(name="ps_y", bufs=2))

        offs_t = keep.tile([P, S // 16], U16)
        pos1_t = keep.tile([P, T // 16], U16)
        pos2_t = keep.tile([P, T // 16], U16)
        x_raw = keep.tile([P, 4, T], F32)
        nc.sync.dma_start(out=x_raw[:], in_=xT.rearrange("(p j) t -> p j t", j=4))
        nc.sync.dma_start(offs_t[:], offs)
        nc.sync.dma_start(pos1_t[:], pos1)
        nc.sync.dma_start(pos2_t[:], pos2)
        w1_raw = {}
        for e in range(E):
            parts = 2 if e == 0 else 1
            width = H // parts
            for i in range(parts):
                tile = raw.tile([P, 4, width], F32, name="raw")
                src = w1[e, :, i * width:(i + 1) * width].rearrange("(p j) c -> p j c", j=4)
                nc.sync.dma_start(out=tile[:], in_=src)
                for q in range(2 // parts):
                    w1_raw[e, i + q] = tile[:, :, q * HALF:(q + 1) * HALF]
        w2_raw = {}
        for a, b, split in W2_LOADS:
            w2_raw[a] = raw.tile([P, 2 * (b - a), 4, N], F32, name="raw")
            src = w2[a:b, :, :].rearrange("e (q p j) n -> p (e q) (j n)", p=P, j=4)
            nc.sync.dma_start(out=w2_raw[a][:].rearrange("p q j n -> p q (j n)"), in_=src)
        gate_t = raw.tile([P, 2, T], F32, name="raw")
        nc.sync.dma_start(out=gate_t[:], in_=gate.rearrange("r p t -> p r t"))

        x_bf = keep.tile([P, T, 4], BF16, align_bytes=64)
        x_words = keep.tile([P, T], U32, align_bytes=64)
        x_bytes = keep.tile([P, T], U8, align_bytes=64)
        nc.gpsimd.memset(x_bytes[:], 0)
        x_src = x_raw[:].rearrange("p j (c i) -> p c j i", i=4)
        x_dst = x_bf[:].rearrange("p (c i) j -> p c j i", i=4)
        nc.vector.tensor_copy(out=x_dst[:, 0:64], in_=x_src[:, 0:64])
        nc.scalar.copy(out=x_dst[:, 64:128], in_=x_src[:, 64:128])
        nc.vector.quantize_mx(out=x_words[:].bitcast(FP8X4), scales=x_bytes[:], in_=x_bf[:].rearrange("p t j -> p (t j)"))
        g_words = keep.tile([P, S], U32, align_bytes=64)
        g_bytes = keep.tile([P, S], U8, align_bytes=64)

        def gather(a, b):
            lst = offs_t[:, a // 16:b // 16]
            nc.vector.tensor_copy(g_words[:, a:b], x_words[:].indirect(lst))
            nc.vector.tensor_copy(g_bytes[:, a:b], x_bytes[:].indirect(lst))

        gathers = {0: (0, 256), 1: (256, 640), 2: (640, 1024)}

        y_all = keep.tile([P, S], F32)

        def cast_w1(e, q):
            grouped = work.tile([P, 4, P, 4], BF16, name="w1_bf", align_bytes=64)
            src = w1_raw[e, q].rearrange("p j (m u v) -> p u m j v", u=2, v=2)
            dst = grouped[:].rearrange("p (u v) m j -> p u m j v", u=2)
            if q == 0 or e == 0:
                nc.scalar.copy(out=dst, in_=src)
            else:
                nc.vector.tensor_copy(out=dst, in_=src)
            return grouped

        def quant_w1(grouped):
            words = work.tile([P, HALF], U32, name="w1_words", align_bytes=64, bufs=4)
            scales = work.tile([P, HALF], U8, name="w1_scales", align_bytes=64, bufs=4)
            nc.vector.quantize_mx(out=words[:].bitcast(FP8X4), scales=scales[:], in_=grouped[:].rearrange("p t m j -> p (t m j)"))
            return words, scales

        def cast_w2(a, b, split):
            grouped = work.tile([P, 2 * (b - a), N, 4], BF16, name="w2_bf", align_bytes=64, bufs=2)
            src = w2_raw[a][:].rearrange("p q j (c i) -> p q c j i", i=4)
            dst = grouped[:].rearrange("p q (c i) j -> p q c j i", i=4)
            if split > 0:
                nc.vector.tensor_copy(out=dst[:, 0:split], in_=src[:, 0:split])
            if split < 2 * (b - a):
                nc.scalar.copy(out=dst[:, split:], in_=src[:, split:])
            return grouped

        def quant_w2(grouped, n):
            words = work.tile([P, n * N], U32, name="w2_words", align_bytes=64, bufs=2)
            scales = work.tile([P, n * N], U8, name="w2_scales", align_bytes=64, bufs=2)
            nc.vector.quantize_mx(out=words[:].bitcast(FP8X4), scales=scales[:], in_=grouped[:].rearrange("p q n j -> p (q n j)"))
            return words, scales

        def layer1(e, w):
            words, scales = w
            bank = ps_a.tile([P, 4 * C], F32, name="h_bank")
            slots = slice(e * C, (e + 1) * C)
            for t in range(4):
                cols = slice(t * P, (t + 1) * P)
                nc.tensor.matmul_mx(
                    out=bank[:, t * C:(t + 1) * C],
                    lhsT=words[:, cols].bitcast(FP8X4), lhsT_scale=scales[:, cols],
                    rhs=g_words[:, slots].bitcast(FP8X4), rhs_scale=g_bytes[:, slots],
                    start=True, stop=True,
                )
            return bank

        def relu(e, banks, h, zero):
            for q in range(2):
                src = banks[q][:].rearrange("p (t n) -> p n t", t=4)
                if q == 1 and e in (1, 3, 5):
                    nc.vector.tensor_scalar(out=h[:, e % 2, q], in0=src, scalar1=zero, scalar2=None, op0=MAX)
                else:
                    nc.scalar.activation(out=h[:, e % 2, q], in_=src, func=RELU, bias=zero)

        def quant_h(h):
            words = hold.tile([P, 4 * C], U32, name="h_words", align_bytes=64)
            scales = hold.tile([P, 4 * C], U8, name="h_scales", align_bytes=64)
            nc.vector.quantize_mx(out=words[:].bitcast(FP8X4), scales=scales[:], in_=h[:].rearrange("p e q n t -> p (e q n t)"))
            return words, scales

        def layer2(e, w, first, hq):
            bank = ps_y.tile([P, C], F32, name="y_bank")
            for q in range(2):
                cols = slice((first + q) * N, (first + q + 1) * N)
                slots = slice((2 * (e % 2) + q) * C, (2 * (e % 2) + q + 1) * C)
                nc.tensor.matmul_mx(
                    out=bank[:],
                    lhsT=w[0][:, cols].bitcast(FP8X4), lhsT_scale=w[1][:, cols],
                    rhs=hq[0][:, slots].bitcast(FP8X4), rhs_scale=hq[1][:, slots],
                    start=(q == 0), stop=(q == 1),
                )
            nc.scalar.copy(out=y_all[:, e * C:(e + 1) * C], in_=bank[:])

        h_codes = []
        banks = {}
        h = None
        for e in range(E):
            if e in gathers:
                gather(*gathers[e])
            halves = [cast_w1(e, q) for q in range(2)]
            if e > 0:
                zero = work.tile([P, 1], F32, name="zero")
                nc.gpsimd.tensor_scalar(out=zero[:], in0=halves[1][:, 3, P - 1, 3:4], scalar1=0.0, scalar2=None, op0=MULT)
                if e % 2 == 1:
                    h = work.tile([P, 2, 2, C, 4], BF16, name="h_bf", align_bytes=64, bufs=2)
                relu(e - 1, banks, h, zero[:])
                if e % 2 == 0:
                    h_codes.append(quant_h(h))
            banks = {}
            for q in (1, 0):
                banks[q] = layer1(e, quant_w1(halves[q]))
        relu(E - 1, banks, h, 0.0)
        for a, b, split in W2_LOADS:
            g = cast_w2(a, b, split)
            if a == 0:
                h_codes.append(quant_h(h))
            w = quant_w2(g, 2 * (b - a))
            for e in range(a, b):
                layer2(e, w, 2 * (e - a), h_codes[e // 2])

        part1 = keep.tile([P, T], F32)
        part2 = keep.tile([P, T], F32)
        result = keep.tile([P, T], F32)
        nc.vector.tensor_tensor(part1[:], y_all[:].indirect(pos1_t[:]), gate_t[:, 0, :], MULT)
        nc.vector.tensor_tensor(part2[:], y_all[:].indirect(pos2_t[:]), gate_t[:, 1, :], MULT)
        nc.vector.tensor_add(result[:], part1[:], part2[:])
        nc.sync.dma_start(out=out, in_=result[:])
